import numpy as np
import ml_dtypes


def mxq(x, axis, fmt="e4m3"):
    dtype, down = {"e4m3": (ml_dtypes.float8_e4m3fn, 7), "e5m2": (ml_dtypes.float8_e5m2, 14)}[fmt]
    v = np.moveaxis(np.asarray(x, np.float32).astype(ml_dtypes.bfloat16).astype(np.float64), axis, -1)
    blocks = v.reshape(v.shape[:-1] + (-1, 32))
    amax = np.abs(blocks).max(-1, keepdims=True)
    byte = np.maximum(np.where(amax > 0, np.frexp(amax)[1] - 1 + 127, 0) - down, 1)
    scale = np.exp2(byte - 127.0)
    codes = (blocks / scale).astype(np.float32).astype(dtype).astype(np.float64)
    return np.moveaxis((codes * scale).reshape(v.shape), -1, axis)


WIDE = False


def mx_kscale(k):
    if not WIDE:
        return np.ones(k)
    levels = np.array([10, -10, 5, -5, 0])
    if k % 512:
        return np.exp2(np.random.permutation(np.resize(levels, k // 32))).repeat(32)
    a = np.empty((k // 512, 16))
    for p in range(k // 512):
        a[p, :8] = np.random.permutation(np.resize(levels, 8))
        for g in range(8):
            far = levels[np.abs(levels - a[p, g]) >= 10]
            a[p, g + 8] = far[np.random.randint(len(far))]
    return np.exp2(a.ravel()).repeat(32)


BF16 = ml_dtypes.bfloat16


def bf(x):
    return np.asarray(x, np.float32).astype(BF16)


def f64(x):
    return np.asarray(x).astype(np.float64)

def planes(Y):
    n, m = Y.shape
    b = f64(bf(Y)).reshape(n // 32, 32, m)
    amax = np.abs(b).max(1)
    byte = np.clip(np.where(amax > 0, np.frexp(amax)[1] - 1 + 127 - 7, 1), 1, 254)
    codes = (b * np.exp2(127.0 - byte)[:, None, :]).reshape(n, m).astype(np.float32).astype(ml_dtypes.float8_e4m3fn).view(np.uint8)
    words = codes.reshape(n // 512, 128, 4, m).transpose(0, 1, 3, 2)
    return np.ascontiguousarray(words), np.ascontiguousarray(byte.astype(np.uint8).reshape(n // 512, 16, m))


B, R, W, C, F, N, K, L = 2, 16, 32, 512, 512, 512, 3, 2
PAD = K // 2


def gelu_tanh(v):
    return 0.5 * v * (1.0 + np.tanh(np.sqrt(2.0 / np.pi) * (v + 0.044715 * (v * v * v))))


def filter_row(rows, taps, width):
    acc = rows[:, :, 0:width, :] * taps[0]
    for v in range(1, taps.shape[0]):
        acc = acc + rows[:, :, v:v + width, :] * taps[v]
    return acc


def depthwise(z, k):
    height, width = z.shape[1], z.shape[2]
    zp = np.pad(z, ((0, 0), (PAD, PAD), (PAD, PAD), (0, 0)))
    acc = filter_row(zp[:, 0:height, :, :], k[0], width)
    for u in range(1, k.shape[0]):
        acc = acc + filter_row(zp[:, u:u + height, :, :], k[u], width)
    return acc


def setup_inputs():
    s, t = mx_kscale(C), mx_kscale(F)
    x = bf(np.random.standard_normal((B, R, W, C)) * s)
    wq = bf(np.random.standard_normal((C, N)) / np.sqrt(C) / s[:, None])
    wz = bf(np.random.standard_normal((C, F)) / np.sqrt(C) / s[:, None])
    wg = bf(np.random.standard_normal((L, C, F)) / np.sqrt(C) / s[None, :, None])
    k = bf(np.random.standard_normal((K, K, F)) / K)
    g = bf((1.0 + 0.1 * np.random.standard_normal(F)) * t)
    wh = bf(1.5 * np.random.standard_normal((F, N)) / np.sqrt(F) / t[:, None])
    return {"x": x, "wq": wq, "wz": wz, "wg": wg, "k": k, "g": g, "wh": wh}


def core(x, wq, wz, wg, k, g, wh):
    xq = mxq(f64(x).reshape(B * R * W, C), 1, "e4m3")
    wgq = mxq(f64(wg), 1, "e4m3")
    z0 = (xq @ mxq(f64(wz), 0, "e4m3")).reshape(B, R, W, F)
    q = (xq @ mxq(f64(wq), 0, "e4m3")).reshape(B, R, W, N)
    a0 = (xq @ wgq[0]).reshape(B, R, W, F)
    a1 = (xq @ wgq[1]).reshape(B, R, W, F)
    z1 = gelu_tanh(depthwise(z0, f64(k)))
    zg = np.mean(z1, axis=(1, 2), keepdims=True)
    ctx = f64(g) * (a0 * z1 + a1 * zg)
    cq = mxq(ctx.reshape(B * R * W, F), 1, "e4m3")
    m = (cq @ mxq(f64(wh), 0, "e4m3")).reshape(B, R, W, N)
    return q * m


def reference(x, wq, wz, wg, k, g, wh):
    R_out = core(x, wq, wz, wg, k, g, wh)
    words, scales = planes(np.moveaxis(R_out, 3, 0).reshape(512, -1))
    return R_out, words, scales

@@ -1,0 +1,458 @@
+from contextlib import ExitStack
+
+import concourse.mybir as mybir
+from concourse.masks import make_identity
+
+F32 = mybir.dt.float32
+BF16 = mybir.dt.bfloat16
+U32 = mybir.dt.uint32
+I32 = mybir.dt.int32
+U8 = mybir.dt.uint8
+FP8X4 = mybir.dt.float8_e4m3fn_x4
+ALU = mybir.AluOpType
+ACT = mybir.ActivationFunctionType
+
+FLOPS = 5 * 2 * 1024 * 512 * 512
+
+P = 128
+B, R, W, C = 2, 16, 32, 512
+T = 4
+POS = 512
+E_COL, O_COL = 0, 576
+WIN_E, WIN_E1, WIN_O1, WIN_O = 0, 64, 512, 576
+M1 = ("V", "V", "V", "V")
+M2 = ("V", "G", "G", "G")
+SD = ("V", "G", "G", "G")
+Y0 = ("V", "V", "V", "V")
+
+
+def tile_focalmodulationtwolevel_x1_kernel(tc, x, wq, wz, wg, k, g, wh, out, words, scales):
+    nc = tc.nc
+    V, S, G, PE = nc.vector, nc.scalar, nc.gpsimd, nc.tensor
+
+    with ExitStack() as ctx:
+        keep = ctx.enter_context(tc.tile_pool(name="keep", bufs=1))
+        work = ctx.enter_context(tc.tile_pool(name="work", bufs=2))
+        psum = ctx.enter_context(tc.psum_pool(name="psum", bufs=1))
+
+        def kt(shape, dtype, name):
+            return keep.tile(shape, dtype, name=name, align_bytes=64)
+
+        def wt(shape, dtype, name, bufs=2):
+            return work.tile(shape, dtype, name=name, tag=name, bufs=bufs, align_bytes=64)
+
+        def bank(name, tag, bufs):
+            return psum.tile([P, 512], F32, name=name, tag=tag, bufs=bufs)
+
+        x_tok = x.rearrange("b r w c -> (b r w) c")
+        x_sb = kt([P, B, 4, C], BF16, "x_sb")
+        taps_bf = kt([P, 3, 3, T], BF16, "taps_bf")
+        gain_bf = kt([P, T], BF16, "gain_bf")
+        raw = {n: kt([P, 4, C], BF16, "raw_" + n) for n in ("z", "g0", "g1", "q", "h")}
+
+        def load_x(b, half):
+            src = x_tok[b * 512 + half * 256 : b * 512 + half * 256 + 256, :]
+            nc.sync.dma_start(out=x_sb[:, b, 2 * half : 2 * half + 2, :], in_=src.rearrange("(q p) c -> p q c", p=P))
+
+        def load_w(n, ap):
+            nc.sync.dma_start(out=raw[n][:], in_=ap.rearrange("(p j) n -> p j n", j=4))
+
+        nc.scalar.dma_start(out=taps_bf[:], in_=k.rearrange("u v (p t) -> p (u v) t", t=T).rearrange("p (u v) t -> p u v t", u=3))
+        nc.scalar.dma_start(out=gain_bf[:], in_=g.rearrange("(p t) -> p t", t=T))
+        load_w("z", wz)
+        load_x(0, 0)
+        load_x(1, 0)
+        load_x(0, 1)
+        load_x(1, 1)
+        load_w("g0", wg[0])
+        load_w("g1", wg[1])
+        load_w("q", wq)
+        load_w("h", wh)
+
+        ident = kt([P, P], F32, "ident")
+        make_identity(nc, ident[:])
+        xg = kt([P, 2, POS, 4], BF16, "xg")
+        xc = kt([P, 1088], U32, "xc")
+        xs = kt([P, 1088], U8, "xs")
+        V.memset(xc[:, 512:576], 0)
+        V.memset(xs[:, 512:576].bitcast(U32), 0)
+        warm = kt([P, 1], F32, "warm")
+        warm2 = kt([P, 1], F32, "warm2")
+        V.memset(warm[:], 0.0)
+        S.activation(out=warm2[:], in_=warm[:], func=ACT.Gelu_apprx_tanh)
+
+        taps = kt([P, 4, 3, T], F32, "taps")
+        outer_half = kt([P, 3, T], F32, "outer_half")
+        gain = kt([P, T], F32, "gain")
+        gain_mean = kt([P, T], F32, "gain_mean")
+
+        def make_taps():
+            V.tensor_tensor(out=outer_half[:], in0=taps_bf[:, 0], in1=taps_bf[:, 2], op=ALU.add)
+            V.tensor_copy(out=taps[:, 0], in_=taps_bf[:, 0])
+            V.tensor_scalar(out=taps[:, 3], in0=taps_bf[:, 2], scalar1=-1.0, scalar2=None, op0=ALU.mult)
+            V.tensor_scalar(out=outer_half[:], in0=outer_half[:], scalar1=0.5, scalar2=None, op0=ALU.mult)
+            V.tensor_copy(out=gain[:], in_=gain_bf[:])
+            V.tensor_scalar(out=gain_mean[:], in0=gain_bf[:], scalar1=1.0 / 512, scalar2=None, op0=ALU.mult)
+            V.scalar_tensor_tensor(out=taps[:, 1], in0=taps_bf[:, 1], scalar=0.5, in1=outer_half[:], op0=ALU.mult, op1=ALU.add)
+            V.scalar_tensor_tensor(out=taps[:, 2], in0=taps_bf[:, 1], scalar=-0.5, in1=outer_half[:], op0=ALU.mult, op1=ALU.add)
+
+        def copy_on(eng, dst, src):
+            if eng is S:
+                S.copy(out=dst, in_=src)
+            elif eng is V:
+                V.tensor_copy(out=dst, in_=src)
+            else:
+                G.tensor_scalar(out=dst, in0=src, scalar1=1.0, scalar2=0.0, op0=ALU.mult, op1=ALU.add)
+
+        xt_tiles = {}
+
+        def x_transpose(q):
+            xt = psum.tile([P, 2, 2, 2, B, W], F32, name="xt%d" % q, tag="a", bufs=4)
+            xt_tiles[q] = xt
+            for b in range(B):
+                blk = x_sb[:, b, q, :].bitcast(F32)
+                for u in range(2):
+                    PE.transpose(xt[:, u, :, :, b, :].rearrange("p a i w -> p i a w"), blk[:, u:256:2], ident[:])
+
+        def x_group(q, eng):
+            dst = xg[:, :, 128 * q : 128 * q + 128, :].rearrange("p a n j -> p a (n j)").bitcast(F32)
+            copy_on(eng, dst.rearrange("p a (n u) -> p a n u", u=2), xt_tiles[q][:].rearrange("p u a i b w -> p a (i b w) u"))
+
+        def x_quant(par):
+            c0 = (E_COL, O_COL)[par]
+            V.quantize_mx(
+                out=xc[:, c0 : c0 + POS].bitcast(FP8X4),
+                scales=xs[:, c0 : c0 + POS],
+                in_=xg[:, par, :, :].rearrange("p n j -> p (n j)"),
+            )
+
+        grp = {n: kt([P, 2048], BF16, "grp_" + n) for n in ("z", "zn", "g0", "g1", "q", "h")}
+        wc = {n: kt([P, 512], U32, "wc_" + n) for n in ("z", "zn", "g0", "g1", "q", "h")}
+        ws = {n: kt([P, 512], U8, "ws_" + n) for n in ("z", "zn", "g0", "g1", "q", "h")}
+
+        def w_group(n, half, eng):
+            if n in ("z", "g0", "g1"):
+                src = raw[n][:].rearrange("p j (m t) -> p t m j", t=T)[:, 2 * half : 2 * half + 2]
+                dst = grp[n][:].rearrange("p (t m j) -> p t m j", t=T, j=4)[:, 2 * half : 2 * half + 2]
+            else:
+                src = raw[n][:].rearrange("p j n -> p n j")[:, 256 * half : 256 * half + 256]
+                dst = grp[n][:].rearrange("p (n j) -> p n j", j=4)[:, 256 * half : 256 * half + 256]
+            copy_on(eng, dst, src)
+
+        def w_negate(half):
+            sl = slice(1024 * half, 1024 * half + 1024)
+            V.tensor_scalar(out=grp["zn"][:, sl], in0=grp["z"][:, sl], scalar1=-1.0, scalar2=None, op0=ALU.mult)
+
+        def w_quant(n, lo, hi):
+            V.quantize_mx(out=wc[n][:, lo:hi].bitcast(FP8X4), scales=ws[n][:, lo:hi], in_=grp[n][:, 4 * lo : 4 * hi])
+
+        def mm(o, n, t, win, start, stop):
+            c = 128 * t
+            PE.matmul_mx(
+                out=o[:],
+                lhsT=wc[n][:, c : c + 128].bitcast(FP8X4),
+                lhsT_scale=ws[n][:, c : c + 128],
+                rhs=xc[:, win : win + POS].bitcast(FP8X4),
+                rhs_scale=xs[:, win : win + POS],
+                start=start,
+                stop=stop,
+            )
+
+        d, prod, y, z1, zsum, gz, a = ({} for i in range(7))
+        tmp, zpart = {}, {}
+        cf = kt([P, T, 2, POS], F32, "cf")
+
+        def grid(ap):
+            return ap.rearrange("p (n w) -> p n w", w=W)
+
+        def transform(t, i):
+            d[t, i] = bank("d%d_%d" % (i, t), "d%d" % i, 1)
+            first, second, name = ((WIN_O1, WIN_O, "zn"), (WIN_E, WIN_O, "z"), (WIN_O, WIN_E, "zn"), (WIN_E, WIN_E1, "zn"))[i]
+            mm(d[t, i], "z", t, first, True, False)
+            mm(d[t, i], name, t, second, False, True)
+
+        def gates(t, which):
+            for par, win in enumerate((WIN_E, WIN_O)):
+                a[t, which, par] = bank("a%d%d_%d" % (which, par, t), "a", 4)
+                mm(a[t, which, par], "g%d" % which, t, win, True, True)
+
+        SPAN = ((slice(1, W), slice(0, W - 1)), (slice(0, W), slice(0, W)), (slice(0, W - 1), slice(1, W)))
+
+        def product(t, i, v):
+            if (t, v) not in prod:
+                prod[t, v] = wt([P, 2, 16, W], F32, "prod%d" % v)
+            dst, src = SPAN[v]
+            S.activation(
+                out=prod[t, v][:, i - 1, :, dst], in_=grid(d[t, i][:])[:, :, src], func=ACT.Copy, scale=taps[:, i, v, t : t + 1]
+            )
+
+        def products(t):
+            for i in (1, 2):
+                product(t, i, 1)
+                if (M1, M2)[i - 1][t] == "G":
+                    product(t, i, 0)
+                    product(t, i, 2)
+
+        def fused(t, i, v, o):
+            dst, src = SPAN[v]
+            V.scalar_tensor_tensor(
+                out=o[:, :, dst], in0=grid(d[t, i][:])[:, :, src], scalar=taps[:, i, v, t : t + 1], in1=o[:, :, dst], op0=ALU.mult, op1=ALU.add
+            )
+
+        def mids(t):
+            acc = prod[t, 1]
+            e1, e2 = M1[t], M2[t]
+            for v in (0, 2):
+                dst = SPAN[v][0]
+                if e1 == e2 == "G":
+                    G.tensor_tensor(out=acc[:, :, :, dst], in0=acc[:, :, :, dst], in1=prod[t, v][:, :, :, dst], op=ALU.add)
+                    continue
+                for i, e in ((1, e1), (2, e2)):
+                    if e == "V":
+                        fused(t, i, v, acc[:, i - 1])
+                    else:
+                        G.tensor_tensor(out=acc[:, i - 1, :, dst], in0=acc[:, i - 1, :, dst], in1=prod[t, v][:, i - 1, :, dst], op=ALU.add)
+
+        def sum_diff(t):
+            acc = prod[t, 1]
+            y[t] = wt([P, 2, 16, W], F32, "y")
+            eng = V if SD[t] == "V" else G
+            eng.tensor_tensor(out=y[t][:, 0], in0=acc[:, 0], in1=acc[:, 1], op=ALU.add)
+            eng.tensor_tensor(out=y[t][:, 1], in0=acc[:, 0], in1=acc[:, 1], op=ALU.subtract)
+
+        def chain(t, v):
+            if Y0[t] == "V":
+                fused(t, 0, v, y[t][:, 0])
+            fused(t, 3, v, y[t][:, 1])
+
+        diag = {}
+
+        def make_diag(t):
+            for v in range(3):
+                diag[t, v] = kt([P, P], F32, "diag%d%d" % (t, v))
+                G.tensor_scalar(out=diag[t, v][:], in0=ident[:], scalar1=taps[:, 0, v, t : t + 1], scalar2=0.0, op0=ALU.mult, op1=ALU.add)
+
+        d0_sb, y0 = {}, {}
+
+        def d0_copy(t):
+            d0_sb[t] = wt([P, 16, W], F32, "d0_sb")
+            S.copy(out=d0_sb[t][:], in_=grid(d[t, 0][:]))
+
+        def y0_taps(t):
+            y0[t] = bank("y0_%d" % t, "a", 4)
+            PE.matmul(out=y0[t][:], lhsT=diag[t, 1][:], rhs=d0_sb[t][:].rearrange("p n w -> p (n w)"), start=True, stop=False)
+            for v in (0, 2):
+                dst, src = SPAN[v]
+                PE.matmul(out=grid(y0[t][:])[:, :, dst], lhsT=diag[t, v][:], rhs=d0_sb[t][:, :, src], start=False, stop=False)
+
+        def y0_sum(t):
+            PE.matmul(out=y0[t][:], lhsT=ident[:], rhs=y[t][:, 0].rearrange("p n w -> p (n w)"), start=False, stop=True)
+
+        def of_batch(ap, b):
+            return ap.rearrange("p (n b w) -> p n b w", b=B, w=W)[:, :, b, :]
+
+        def gelu(t, b):
+            if b == 0:
+                z1[t] = wt([P, 2 * POS], F32, "z1")
+                zsum[t] = wt([P, B], F32, "zsum")
+                gz[t] = wt([P, B], F32, "gz")
+            if Y0[t] == "PE":
+                for par, src in enumerate((y0[t][:], y[t][:, 1].rearrange("p n w -> p (n w)"))):
+                    if (t, b) not in zpart:
+                        zpart[t, b] = wt([P, 2], F32, "zpart%d" % b)
+                    S.activation(
+                        out=of_batch(z1[t][:, par * POS : (par + 1) * POS], b),
+                        in_=of_batch(src, b),
+                        func=ACT.Gelu_apprx_tanh,
+                        accum_out=zpart[t, b][:, par : par + 1],
+                    )
+                V.tensor_tensor(out=zsum[t][:, b : b + 1], in0=zpart[t, b][:, 0:1], in1=zpart[t, b][:, 1:2], op=ALU.add)
+                return
+            S.activation(
+                out=of_batch(z1[t][:], b),
+                in_=of_batch(y[t][:].rearrange("p a n w -> p (a n w)"), b),
+                func=ACT.Gelu_apprx_tanh,
+                accum_out=zsum[t][:, b : b + 1],
+            )
+
+        def glob_gain(t):
+            S.activation(out=gz[t][:], in_=zsum[t][:], func=ACT.Copy, scale=gain_mean[:, t : t + 1])
+
+        def local(t, par):
+            if par == 0:
+                tmp[t] = wt([P, 2, POS], F32, "tmp", bufs=1)
+            V.scalar_tensor_tensor(
+                out=tmp[t][:, par], in0=z1[t][:, par * POS : (par + 1) * POS], scalar=gain[:, t : t + 1], in1=a[t, 0, par][:], op0=ALU.mult, op1=ALU.mult
+            )
+
+        def combine(t, par, b):
+            V.scalar_tensor_tensor(
+                out=of_batch(cf[:, t, par, :], b), in0=of_batch(a[t, 1, par][:], b), scalar=gz[t][:, b : b + 1], in1=of_batch(tmp[t][:, par], b), op0=ALU.mult, op1=ALU.add
+            )
+
+        q_sb = kt([P, 2, 4, C], F32, "q_sb")
+        qb = {}
+
+        def q_mm(par, h):
+            c0 = (E_COL, O_COL)[par] + 128 * h
+            qb[par, h] = bank("q%d%d" % (par, h), "a", 4)
+            PE.matmul_mx(
+                out=qb[par, h][:],
+                lhsT=xc[:, c0 : c0 + 128].bitcast(FP8X4),
+                lhsT_scale=xs[:, c0 : c0 + 128],
+                rhs=wc["q"][:].bitcast(FP8X4),
+                rhs_scale=ws["q"][:],
+                start=True,
+                stop=True,
+            )
+
+        def q_copy(par, h, eng):
+            copy_on(eng, q_sb[:, par, h, :], qb[par, h][:])
+
+        ctxg = kt([P, 2, POS, 4], BF16, "ctxg")
+        cc = kt([P, 2, POS], U32, "cc")
+        cs = kt([P, 2, POS], U8, "cs")
+        og, o_sb, m_bank, ot = {}, {}, {}, {}
+
+        def ctx_group(par, h, eng):
+            sl = slice(128 * h, 128 * h + 128)
+            copy_on(eng, ctxg[:, par, sl, :], cf[:, :, par, sl].rearrange("p t n -> p n t"))
+
+        def ctx_quant(par, h):
+            sl = slice(128 * h, 128 * h + 128)
+            V.quantize_mx(out=cc[:, par, sl].bitcast(FP8X4), scales=cs[:, par, sl], in_=ctxg[:, par, sl, :].rearrange("p n t -> p (n t)"))
+
+        def m_mm(par, h):
+            sl = slice(128 * h, 128 * h + 128)
+            m_bank[par, h] = bank("m%d%d" % (par, h), "a", 4)
+            PE.matmul_mx(
+                out=m_bank[par, h][:],
+                lhsT=cc[:, par, sl].bitcast(FP8X4),
+                lhsT_scale=cs[:, par, sl],
+                rhs=wc["h"][:].bitcast(FP8X4),
+                rhs_scale=ws["h"][:],
+                start=True,
+                stop=True,
+            )
+
+        def modulate(par, h):
+            o = wt([P, C], F32, "o", bufs=4)
+            o_sb[par, h] = o
+            V.tensor_tensor(out=o[:], in0=m_bank[par, h][:], in1=q_sb[:, par, h, :], op=ALU.mult)
+            for i in range(2):
+                for b in range(B):
+                    lo = 64 * i + 32 * b
+                    nc.sync.dma_start(out=out[b, 2 * (2 * h + i) + par, :, :], in_=o[lo : lo + 32, :])
+
+        def turn(par, h):
+            ot[par, h] = psum.tile([P, T, 2, B, W], F32, name="ot%d%d" % (par, h), tag="d%d" % (2 * (h % 2) + par), bufs=1)
+            for t in range(T):
+                PE.transpose(ot[par, h][:, t].rearrange("p i b w -> p (i b w)"), o_sb[par, h][:, t:C:4], ident[:])
+
+        def out_group(par, h, eng):
+            if h not in og:
+                og[h] = kt([P, B, 2, 2, W, 4], BF16, "og%d" % h)
+            for b in range(B):
+                copy_on(eng, og[h][:, b, :, par, :, :], ot[par, h][:, :, :, b, :].rearrange("p t i w -> p i w t"))
+
+        def planes(h):
+            pc = kt([P, 256], U32, "pc%d" % h)
+            ps = kt([P, 256], U8, "ps%d" % h)
+            V.quantize_mx(out=pc[:].bitcast(FP8X4), scales=ps[:], in_=og[h][:].rearrange("p b i a w t -> p (b i a w t)"))
+            w_dst = words[0].rearrange("p (b n) t -> p b (n t)", b=B)[:, :, 512 * h : 512 * h + 512].bitcast(I32)
+            nc.sync.dma_start(out=w_dst, in_=pc[:].rearrange("p (b n) -> p b n", b=B).bitcast(I32))
+            s_dst = scales[0].rearrange("q (b n) -> q b n", b=B)[:, :, 128 * h : 128 * h + 128].bitcast(I32)
+            for quad in range(4):
+                nc.sync.dma_start(
+                    out=s_dst[4 * quad : 4 * quad + 4],
+                    in_=ps[32 * quad : 32 * quad + 4, :].rearrange("q (b n) -> q b n", b=B).bitcast(I32),
+                )
+
+        make_taps()
+        w_group("z", 0, V)
+        w_group("z", 1, S)
+
+        w_quant("z", 0, 256)
+        w_negate(0)
+        w_quant("zn", 0, 256)
+        for q in range(4):
+            x_transpose(q)
+        x_group(0, S)
+        x_group(1, V)
+        x_group(2, S)
+        x_group(3, V)
+        x_quant(0)
+        x_quant(1)
+        for i in (1, 2, 0, 3):
+            transform(0, i)
+        products(0)
+        mids(0)
+        sum_diff(0)
+        w_quant("z", 256, 512)
+        w_negate(1)
+        w_quant("zn", 256, 512)
+        transform(1, 1)
+        transform(1, 2)
+        products(1)
+        mids(1)
+        sum_diff(1)
+        w_group("g0", 0, S)
+        w_group("g0", 1, V)
+        w_quant("g0", 0, 512)
+        w_group("g1", 0, V)
+        w_group("g1", 1, V)
+        w_quant("g1", 0, 512)
+        for t in range(T):
+            if Y0[t] == "PE":
+                d0_copy(t)
+                y0_taps(t)
+            for v in (1, 0, 2):
+                chain(t, v)
+            if Y0[t] == "PE":
+                y0_sum(t)
+            gates(t, 0)
+            gates(t, 1)
+            if t + 1 < T:
+                transform(t + 1, 0)
+                transform(t + 1, 3)
+            for b in range(B):
+                gelu(t, b)
+            glob_gain(t)
+            if t + 2 < T:
+                transform(t + 2, 1)
+                transform(t + 2, 2)
+                products(t + 2)
+                mids(t + 2)
+                sum_diff(t + 2)
+            for par in range(2):
+                local(t, par)
+            for par in range(2):
+                for b in range(B):
+                    combine(t, par, b)
+            if t == 0:
+                w_group("q", 0, S)
+                w_group("q", 1, S)
+                w_quant("q", 0, 512)
+                for h in range(4):
+                    q_mm(0, h)
+                    q_copy(0, h, S)
+            if t == 1:
+                w_group("h", 0, S)
+                w_group("h", 1, S)
+                w_quant("h", 0, 512)
+                for h in range(4):
+                    q_mm(1, h)
+                    q_copy(1, h, S)
+        blocks = [(par, h) for h in range(4) for par in range(2)]
+        for i in range(len(blocks) + 3):
+            if i < 8:
+                ctx_group(*blocks[i], (S, V, G, S, V, G, S, V)[i])
+                ctx_quant(*blocks[i])
+                m_mm(*blocks[i])
+            if 0 <= i - 1 < 8:
+                modulate(*blocks[i - 1])
+            if 0 <= i - 2 < 8:
+                turn(*blocks[i - 2])
+                out_group(*blocks[i - 2], S)
+            if i >= 3 and blocks[i - 3][0] == 1:
+                planes(blocks[i - 3][1])

@@ -20,10 +20,12 @@ T = 4
 POS = 512
 E_COL, O_COL = 0, 576
 WIN_E, WIN_E1, WIN_O1, WIN_O = 0, 64, 512, 576
-M1 = ("V", "V", "V", "V")
+M1 = ("V", "V", "G", "V")
 M2 = ("V", "G", "G", "G")
 SD = ("V", "G", "G", "G")
 Y0 = ("V", "V", "V", "V")
+Q_BANK = (('a0', 'a1', 'a0', 'a1'), ('a0', 'a1', 'a0', 'a1'))
+Y0_BANK = "d0"
 
 
 def tile_focalmodulationtwolevel_x1_kernel(tc, x, wq, wz, wg, k, g, wh, out, words, scales):
@@ -34,6 +36,7 @@ def tile_focalmodulationtwolevel_x1_kernel(tc, x, wq, wz, wg, k, g, wh, out, wor
         keep = ctx.enter_context(tc.tile_pool(name="keep", bufs=1))
         work = ctx.enter_context(tc.tile_pool(name="work", bufs=2))
         psum = ctx.enter_context(tc.psum_pool(name="psum", bufs=1))
+        ctx.enter_context(tc.manual_schedule())
 
         def kt(shape, dtype, name):
             return keep.tile(shape, dtype, name=name, align_bytes=64)
@@ -64,9 +67,9 @@ def tile_focalmodulationtwolevel_x1_kernel(tc, x, wq, wz, wg, k, g, wh, out, wor
         load_x(1, 0)
         load_x(0, 1)
         load_x(1, 1)
+        load_w("q", wq)
         load_w("g0", wg[0])
         load_w("g1", wg[1])
-        load_w("q", wq)
         load_w("h", wh)
 
         ident = kt([P, P], F32, "ident")
@@ -107,7 +110,7 @@ def tile_focalmodulationtwolevel_x1_kernel(tc, x, wq, wz, wg, k, g, wh, out, wor
         xt_tiles = {}
 
         def x_transpose(q):
-            xt = psum.tile([P, 2, 2, 2, B, W], F32, name="xt%d" % q, tag="a", bufs=4)
+            xt = psum.tile([P, 2, 2, 2, B, W], F32, name="xt%d" % q, tag="a%d" % q, bufs=1)
             xt_tiles[q] = xt
             for b in range(B):
                 blk = x_sb[:, b, q, :].bitcast(F32)
@@ -166,14 +169,14 @@ def tile_focalmodulationtwolevel_x1_kernel(tc, x, wq, wz, wg, k, g, wh, out, wor
             return ap.rearrange("p (n w) -> p n w", w=W)
 
         def transform(t, i):
-            d[t, i] = bank("d%d_%d" % (i, t), "d%d" % i, 1)
+            d[t, i] = bank("d%d_%d" % (i, t), "a%d" % (i + 1) if t == 1 and i in (1, 2) else "d%d" % i, 1)
             first, second, name = ((WIN_O1, WIN_O, "zn"), (WIN_E, WIN_O, "z"), (WIN_O, WIN_E, "zn"), (WIN_E, WIN_E1, "zn"))[i]
             mm(d[t, i], "z", t, first, True, False)
             mm(d[t, i], name, t, second, False, True)
 
-        def gates(t, which):
-            for par, win in enumerate((WIN_E, WIN_O)):
-                a[t, which, par] = bank("a%d%d_%d" % (which, par, t), "a", 4)
+        def gate(t, which, par):
+            for win in ((WIN_E, WIN_O)[par],):
+                a[t, which, par] = bank("a%d%d_%d" % (which, par, t), "a%d" % (2 * which + par), 1)
                 mm(a[t, which, par], "g%d" % which, t, win, True, True)
 
         SPAN = ((slice(1, W), slice(0, W - 1)), (slice(0, W), slice(0, W)), (slice(0, W - 1), slice(1, W)))
@@ -199,31 +202,23 @@ def tile_focalmodulationtwolevel_x1_kernel(tc, x, wq, wz, wg, k, g, wh, out, wor
                 out=o[:, :, dst], in0=grid(d[t, i][:])[:, :, src], scalar=taps[:, i, v, t : t + 1], in1=o[:, :, dst], op0=ALU.mult, op1=ALU.add
             )
 
-        def mids(t):
+        def mid(t, i, v):
             acc = prod[t, 1]
-            e1, e2 = M1[t], M2[t]
-            for v in (0, 2):
-                dst = SPAN[v][0]
-                if e1 == e2 == "G":
-                    G.tensor_tensor(out=acc[:, :, :, dst], in0=acc[:, :, :, dst], in1=prod[t, v][:, :, :, dst], op=ALU.add)
-                    continue
-                for i, e in ((1, e1), (2, e2)):
-                    if e == "V":
-                        fused(t, i, v, acc[:, i - 1])
-                    else:
-                        G.tensor_tensor(out=acc[:, i - 1, :, dst], in0=acc[:, i - 1, :, dst], in1=prod[t, v][:, i - 1, :, dst], op=ALU.add)
+            dst = SPAN[v][0]
+            if (M1, M2)[i - 1][t] == "V":
+                fused(t, i, v, acc[:, i - 1])
+            else:
+                G.tensor_tensor(out=acc[:, i - 1, :, dst], in0=acc[:, i - 1, :, dst], in1=prod[t, v][:, i - 1, :, dst], op=ALU.add)
 
-        def sum_diff(t):
+        def sum_diff(t, half):
             acc = prod[t, 1]
-            y[t] = wt([P, 2, 16, W], F32, "y")
+            if t not in y:
+                y[t] = wt([P, 2, 16, W], F32, "y")
             eng = V if SD[t] == "V" else G
-            eng.tensor_tensor(out=y[t][:, 0], in0=acc[:, 0], in1=acc[:, 1], op=ALU.add)
-            eng.tensor_tensor(out=y[t][:, 1], in0=acc[:, 0], in1=acc[:, 1], op=ALU.subtract)
+            eng.tensor_tensor(out=y[t][:, half], in0=acc[:, 0], in1=acc[:, 1], op=(ALU.add, ALU.subtract)[half])
 
-        def chain(t, v):
-            if Y0[t] == "V":
-                fused(t, 0, v, y[t][:, 0])
-            fused(t, 3, v, y[t][:, 1])
+        def chain(t, half, v):
+            fused(t, (0, 3)[half], v, y[t][:, half])
 
         diag = {}
 
@@ -239,7 +234,7 @@ def tile_focalmodulationtwolevel_x1_kernel(tc, x, wq, wz, wg, k, g, wh, out, wor
             S.copy(out=d0_sb[t][:], in_=grid(d[t, 0][:]))
 
         def y0_taps(t):
-            y0[t] = bank("y0_%d" % t, "a", 4)
+            y0[t] = bank("y0_%d" % t, Y0_BANK, 1)
             PE.matmul(out=y0[t][:], lhsT=diag[t, 1][:], rhs=d0_sb[t][:].rearrange("p n w -> p (n w)"), start=True, stop=False)
             for v in (0, 2):
                 dst, src = SPAN[v]
@@ -252,7 +247,7 @@ def tile_focalmodulationtwolevel_x1_kernel(tc, x, wq, wz, wg, k, g, wh, out, wor
             return ap.rearrange("p (n b w) -> p n b w", b=B, w=W)[:, :, b, :]
 
         def gelu(t, b):
-            if b == 0:
+            if t not in z1:
                 z1[t] = wt([P, 2 * POS], F32, "z1")
                 zsum[t] = wt([P, B], F32, "zsum")
                 gz[t] = wt([P, B], F32, "gz")
@@ -266,7 +261,6 @@ def tile_focalmodulationtwolevel_x1_kernel(tc, x, wq, wz, wg, k, g, wh, out, wor
                         func=ACT.Gelu_apprx_tanh,
                         accum_out=zpart[t, b][:, par : par + 1],
                     )
-                V.tensor_tensor(out=zsum[t][:, b : b + 1], in0=zpart[t, b][:, 0:1], in1=zpart[t, b][:, 1:2], op=ALU.add)
                 return
             S.activation(
                 out=of_batch(z1[t][:], b),
@@ -275,11 +269,14 @@ def tile_focalmodulationtwolevel_x1_kernel(tc, x, wq, wz, wg, k, g, wh, out, wor
                 accum_out=zsum[t][:, b : b + 1],
             )
 
+        def zadd(t, b):
+            V.tensor_tensor(out=zsum[t][:, b : b + 1], in0=zpart[t, b][:, 0:1], in1=zpart[t, b][:, 1:2], op=ALU.add)
+
         def glob_gain(t):
             S.activation(out=gz[t][:], in_=zsum[t][:], func=ACT.Copy, scale=gain_mean[:, t : t + 1])
 
         def local(t, par):
-            if par == 0:
+            if t not in tmp:
                 tmp[t] = wt([P, 2, POS], F32, "tmp", bufs=1)
             V.scalar_tensor_tensor(
                 out=tmp[t][:, par], in0=z1[t][:, par * POS : (par + 1) * POS], scalar=gain[:, t : t + 1], in1=a[t, 0, par][:], op0=ALU.mult, op1=ALU.mult
@@ -295,7 +292,7 @@ def tile_focalmodulationtwolevel_x1_kernel(tc, x, wq, wz, wg, k, g, wh, out, wor
 
         def q_mm(par, h):
             c0 = (E_COL, O_COL)[par] + 128 * h
-            qb[par, h] = bank("q%d%d" % (par, h), "a", 4)
+            qb[par, h] = bank("q%d%d" % (par, h), Q_BANK[par][h], 1)
             PE.matmul_mx(
                 out=qb[par, h][:],
                 lhsT=xc[:, c0 : c0 + 128].bitcast(FP8X4),
@@ -324,7 +321,7 @@ def tile_focalmodulationtwolevel_x1_kernel(tc, x, wq, wz, wg, k, g, wh, out, wor
 
         def m_mm(par, h):
             sl = slice(128 * h, 128 * h + 128)
-            m_bank[par, h] = bank("m%d%d" % (par, h), "a", 4)
+            m_bank[par, h] = bank("m%d%d" % (par, h), "a%d" % (2 * (h % 2) + par), 1)
             PE.matmul_mx(
                 out=m_bank[par, h][:],
                 lhsT=cc[:, par, sl].bitcast(FP8X4),
@@ -369,90 +366,233 @@ def tile_focalmodulationtwolevel_x1_kernel(tc, x, wq, wz, wg, k, g, wh, out, wor
                 )
 
         make_taps()
-        w_group("z", 0, V)
         w_group("z", 1, S)
-
-        w_quant("z", 0, 256)
+        w_group("z", 0, V)
+        x_transpose(1)
         w_negate(0)
-        w_quant("zn", 0, 256)
-        for q in range(4):
-            x_transpose(q)
+        w_quant("z", 0, 256)
+        x_transpose(0)
+        w_quant("z", 256, 512)
+        x_transpose(2)
+        w_negate(1)
         x_group(0, S)
         x_group(1, V)
+        x_transpose(3)
         x_group(2, S)
         x_group(3, V)
+        w_group("q", 1, S)
         x_quant(0)
         x_quant(1)
-        for i in (1, 2, 0, 3):
-            transform(0, i)
-        products(0)
-        mids(0)
-        sum_diff(0)
-        w_quant("z", 256, 512)
-        w_negate(1)
+        w_group("q", 0, S)
+        transform(0, 1)
         w_quant("zn", 256, 512)
-        transform(1, 1)
+        w_quant("zn", 0, 256)
+        transform(0, 2)
+        w_group("g1", 1, G)
+        product(0, 1, 1)
         transform(1, 2)
-        products(1)
-        mids(1)
-        sum_diff(1)
+        product(0, 2, 1)
+        mid(0, 1, 0)
+        w_group("g0", 1, S)
+        w_group("g1", 0, G)
+        mid(0, 2, 0)
+        mid(0, 1, 2)
+        mid(0, 2, 2)
         w_group("g0", 0, S)
-        w_group("g0", 1, V)
-        w_quant("g0", 0, 512)
-        w_group("g1", 0, V)
-        w_group("g1", 1, V)
+        w_quant("q", 0, 512)
+        transform(2, 2)
+        sum_diff(0, 1)
+        transform(0, 3)
+        product(1, 2, 1)
         w_quant("g1", 0, 512)
-        for t in range(T):
-            if Y0[t] == "PE":
-                d0_copy(t)
-                y0_taps(t)
-            for v in (1, 0, 2):
-                chain(t, v)
-            if Y0[t] == "PE":
-                y0_sum(t)
-            gates(t, 0)
-            gates(t, 1)
-            if t + 1 < T:
-                transform(t + 1, 0)
-                transform(t + 1, 3)
-            for b in range(B):
-                gelu(t, b)
-            glob_gain(t)
-            if t + 2 < T:
-                transform(t + 2, 1)
-                transform(t + 2, 2)
-                products(t + 2)
-                mids(t + 2)
-                sum_diff(t + 2)
-            for par in range(2):
-                local(t, par)
-            for par in range(2):
-                for b in range(B):
-                    combine(t, par, b)
-            if t == 0:
-                w_group("q", 0, S)
-                w_group("q", 1, S)
-                w_quant("q", 0, 512)
-                for h in range(4):
-                    q_mm(0, h)
-                    q_copy(0, h, S)
-            if t == 1:
-                w_group("h", 0, S)
-                w_group("h", 1, S)
-                w_quant("h", 0, 512)
-                for h in range(4):
-                    q_mm(1, h)
-                    q_copy(1, h, S)
-        blocks = [(par, h) for h in range(4) for par in range(2)]
-        for i in range(len(blocks) + 3):
-            if i < 8:
-                ctx_group(*blocks[i], (S, V, G, S, V, G, S, V)[i])
-                ctx_quant(*blocks[i])
-                m_mm(*blocks[i])
-            if 0 <= i - 1 < 8:
-                modulate(*blocks[i - 1])
-            if 0 <= i - 2 < 8:
-                turn(*blocks[i - 2])
-                out_group(*blocks[i - 2], S)
-            if i >= 3 and blocks[i - 3][0] == 1:
-                planes(blocks[i - 3][1])
+        q_mm(0, 1)
+        product(1, 2, 2)
+        transform(1, 1)
+        w_quant("g0", 0, 512)
+        product(1, 2, 0)
+        q_mm(0, 0)
+        sum_diff(0, 0)
+        product(1, 1, 1)
+        gate(0, 1, 1)
+        mid(1, 2, 0)
+        chain(0, 1, 1)
+        transform(0, 0)
+        product(2, 2, 0)
+        mid(1, 1, 0)
+        transform(2, 1)
+        q_copy(0, 1, S)
+        chain(0, 1, 0)
+        mid(1, 2, 2)
+        product(2, 1, 1)
+        mid(1, 1, 2)
+        product(2, 1, 0)
+        chain(0, 0, 1)
+        sum_diff(1, 1)
+        product(2, 1, 2)
+        chain(0, 1, 2)
+        product(2, 2, 1)
+        chain(0, 0, 0)
+        transform(1, 3)
+        sum_diff(1, 0)
+        q_copy(0, 0, S)
+        transform(3, 1)
+        chain(0, 0, 2)
+        product(2, 2, 2)
+        chain(1, 1, 1)
+        mid(2, 2, 0)
+        transform(1, 0)
+        gelu(0, 0)
+        q_mm(0, 2)
+        chain(1, 1, 0)
+        gate(0, 1, 0)
+        mid(2, 1, 0)
+        q_copy(0, 2, S)
+        transform(3, 2)
+        chain(1, 0, 1)
+        gelu(0, 1)
+        q_mm(0, 3)
+        chain(1, 1, 2)
+        gate(0, 0, 0)
+        mid(2, 2, 2)
+        chain(1, 0, 0)
+        transform(2, 3)
+        glob_gain(0)
+        product(3, 1, 1)
+        local(0, 0)
+        q_copy(0, 3, S)
+        mid(2, 1, 2)
+        chain(1, 0, 2)
+        q_mm(1, 0)
+        product(3, 2, 1)
+        gate(0, 0, 1)
+        mid(3, 1, 0)
+        transform(2, 0)
+        q_copy(1, 0, S)
+        sum_diff(2, 0)
+        local(0, 1)
+        product(3, 2, 2)
+        combine(0, 0, 0)
+        gate(1, 0, 0)
+        combine(0, 1, 1)
+        q_mm(1, 1)
+        gelu(1, 1)
+        sum_diff(2, 1)
+        combine(0, 0, 1)
+        mid(3, 1, 2)
+        product(3, 2, 0)
+        chain(2, 0, 1)
+        gelu(1, 0)
+        mid(3, 2, 0)
+        chain(2, 1, 1)
+        w_group("h", 0, S)
+        combine(0, 1, 0)
+        chain(2, 0, 0)
+        mid(3, 2, 2)
+        chain(2, 1, 0)
+        q_copy(1, 1, S)
+        local(1, 0)
+        glob_gain(1)
+        sum_diff(3, 0)
+        gate(1, 0, 1)
+        chain(2, 0, 2)
+        gate(1, 1, 1)
+        q_mm(1, 2)
+        local(1, 1)
+        transform(3, 0)
+        sum_diff(3, 1)
+        chain(2, 1, 2)
+        gate(1, 1, 0)
+        combine(1, 1, 0)
+        transform(3, 3)
+        gelu(2, 0)
+        chain(3, 0, 1)
+        q_mm(1, 3)
+        combine(1, 1, 1)
+        gelu(2, 1)
+        combine(1, 0, 0)
+        chain(3, 0, 0)
+        q_copy(1, 2, S)
+        chain(3, 1, 1)
+        q_copy(1, 3, S)
+        gate(2, 0, 0)
+        combine(1, 0, 1)
+        gate(2, 1, 1)
+        glob_gain(2)
+        w_group("h", 1, S)
+        chain(3, 1, 0)
+        gate(2, 0, 1)
+        gate(2, 1, 0)
+        chain(3, 0, 2)
+        local(2, 0)
+        local(2, 1)
+        chain(3, 1, 2)
+        gate(3, 0, 1)
+        gate(3, 0, 0)
+        combine(2, 1, 1)
+        gelu(3, 0)
+        combine(2, 1, 0)
+        combine(2, 0, 0)
+        gelu(3, 1)
+        combine(2, 0, 1)
+        w_quant("h", 0, 512)
+        gate(3, 1, 0)
+        gate(3, 1, 1)
+        glob_gain(3)
+        local(3, 0)
+        local(3, 1)
+        combine(3, 0, 1)
+        combine(3, 0, 0)
+        combine(3, 1, 0)
+        ctx_group(0, 0, S)
+        ctx_group(0, 1, G)
+        combine(3, 1, 1)
+        ctx_group(1, 1, S)
+        ctx_group(1, 0, V)
+        ctx_group(1, 2, G)
+        ctx_group(0, 3, S)
+        ctx_quant(0, 0)
+        ctx_quant(0, 1)
+        m_mm(0, 0)
+        ctx_quant(1, 1)
+        ctx_quant(1, 0)
+        ctx_group(0, 2, V)
+        m_mm(1, 0)
+        modulate(0, 0)
+        m_mm(0, 1)
+        m_mm(1, 1)
+        ctx_quant(0, 2)
+        modulate(1, 0)
+        turn(0, 0)
+        modulate(0, 1)
+        turn(1, 0)
+        out_group(0, 0, S)
+        ctx_quant(0, 3)
+        modulate(1, 1)
+        m_mm(0, 2)
+        out_group(1, 0, S)
+        m_mm(0, 3)
+        ctx_group(1, 3, V)
+        turn(0, 1)
+        planes(0)
+        ctx_quant(1, 2)
+        turn(1, 1)
+        ctx_quant(1, 3)
+        modulate(0, 2)
+        m_mm(1, 2)
+        out_group(1, 1, S)
+        m_mm(1, 3)
+        modulate(1, 2)
+        turn(0, 2)
+        out_group(0, 1, S)
+        modulate(0, 3)
+        turn(1, 2)
+        out_group(0, 2, S)
+        turn(0, 3)
+        modulate(1, 3)
+        out_group(1, 2, S)
+        planes(1)
+        turn(1, 3)
+        out_group(0, 3, S)
+        planes(2)
+        out_group(1, 3, S)
+        planes(3)

@@ -20,12 +20,12 @@ T = 4
 POS = 512
 E_COL, O_COL = 0, 576
 WIN_E, WIN_E1, WIN_O1, WIN_O = 0, 64, 512, 576
-M1 = ("V", "V", "G", "V")
+M1 = ("V", "V", "V", "G")
 M2 = ("V", "G", "G", "G")
 SD = ("V", "G", "G", "G")
-Y0 = ("V", "V", "V", "V")
+Y0 = ("V", "V", "V", "PE")
 Q_BANK = (('a0', 'a1', 'a0', 'a1'), ('a0', 'a1', 'a0', 'a1'))
-Y0_BANK = "d0"
+Y0_BANK = "d1"
 
 
 def tile_focalmodulationtwolevel_x1_kernel(tc, x, wq, wz, wg, k, g, wh, out, words, scales):
@@ -36,7 +36,7 @@ def tile_focalmodulationtwolevel_x1_kernel(tc, x, wq, wz, wg, k, g, wh, out, wor
         keep = ctx.enter_context(tc.tile_pool(name="keep", bufs=1))
         work = ctx.enter_context(tc.tile_pool(name="work", bufs=2))
         psum = ctx.enter_context(tc.psum_pool(name="psum", bufs=1))
-        ctx.enter_context(tc.manual_schedule())
+        ctx.enter_context(tc.manual_schedule(engines={mybir.EngineType.PE, mybir.EngineType.Activation, mybir.EngineType.DVE, mybir.EngineType.Pool}))
 
         def kt(shape, dtype, name):
             return keep.tile(shape, dtype, name=name, align_bytes=64)
@@ -169,7 +169,7 @@ def tile_focalmodulationtwolevel_x1_kernel(tc, x, wq, wz, wg, k, g, wh, out, wor
             return ap.rearrange("p (n w) -> p n w", w=W)
 
         def transform(t, i):
-            d[t, i] = bank("d%d_%d" % (i, t), "a%d" % (i + 1) if t == 1 and i in (1, 2) else "d%d" % i, 1)
+            d[t, i] = bank("d%d_%d" % (i, t), "a%d" % (i + 1) if t == 1 and i in (1, 2) else "d2" if i == 0 and Y0[t] == "PE" else "d%d" % i, 1)
             first, second, name = ((WIN_O1, WIN_O, "zn"), (WIN_E, WIN_O, "z"), (WIN_O, WIN_E, "zn"), (WIN_E, WIN_E1, "zn"))[i]
             mm(d[t, i], "z", t, first, True, False)
             mm(d[t, i], name, t, second, False, True)
@@ -333,18 +333,21 @@ def tile_focalmodulationtwolevel_x1_kernel(tc, x, wq, wz, wg, k, g, wh, out, wor
             )
 
         def modulate(par, h):
-            o = wt([P, C], F32, "o", bufs=4)
-            o_sb[par, h] = o
-            V.tensor_tensor(out=o[:], in0=m_bank[par, h][:], in1=q_sb[:, par, h, :], op=ALU.mult)
+            if h not in o_sb:
+                o_sb[h] = wt([P, 2, C], F32, "o", bufs=4)
+            V.tensor_tensor(out=o_sb[h][:, par, :], in0=m_bank[par, h][:], in1=q_sb[:, par, h, :], op=ALU.mult)
+
+        def store_out(h):
             for i in range(2):
                 for b in range(B):
                     lo = 64 * i + 32 * b
-                    nc.sync.dma_start(out=out[b, 2 * (2 * h + i) + par, :, :], in_=o[lo : lo + 32, :])
+                    dst = out[b, 4 * h + 2 * i : 4 * h + 2 * i + 2, :, :].rearrange("a w n -> w a n")
+                    nc.sync.dma_start(out=dst, in_=o_sb[h][lo : lo + 32, :, :])
 
         def turn(par, h):
             ot[par, h] = psum.tile([P, T, 2, B, W], F32, name="ot%d%d" % (par, h), tag="d%d" % (2 * (h % 2) + par), bufs=1)
             for t in range(T):
-                PE.transpose(ot[par, h][:, t].rearrange("p i b w -> p (i b w)"), o_sb[par, h][:, t:C:4], ident[:])
+                PE.transpose(ot[par, h][:, t].rearrange("p i b w -> p (i b w)"), o_sb[h][:, par, t:C:4], ident[:])
 
         def out_group(par, h, eng):
             if h not in og:
@@ -352,40 +355,47 @@ def tile_focalmodulationtwolevel_x1_kernel(tc, x, wq, wz, wg, k, g, wh, out, wor
             for b in range(B):
                 copy_on(eng, og[h][:, b, :, par, :, :], ot[par, h][:, :, :, b, :].rearrange("p t i w -> p i w t"))
 
+        pc = kt([P, B, 512], U32, "pc")
+        ps = kt([P, B, 512], U8, "ps")
+
         def planes(h):
-            pc = kt([P, 256], U32, "pc%d" % h)
-            ps = kt([P, 256], U8, "ps%d" % h)
-            V.quantize_mx(out=pc[:].bitcast(FP8X4), scales=ps[:], in_=og[h][:].rearrange("p b i a w t -> p (b i a w t)"))
-            w_dst = words[0].rearrange("p (b n) t -> p b (n t)", b=B)[:, :, 512 * h : 512 * h + 512].bitcast(I32)
-            nc.sync.dma_start(out=w_dst, in_=pc[:].rearrange("p (b n) -> p b n", b=B).bitcast(I32))
-            s_dst = scales[0].rearrange("q (b n) -> q b n", b=B)[:, :, 128 * h : 128 * h + 128].bitcast(I32)
-            for quad in range(4):
-                nc.sync.dma_start(
-                    out=s_dst[4 * quad : 4 * quad + 4],
-                    in_=ps[32 * quad : 32 * quad + 4, :].rearrange("q (b n) -> q b n", b=B).bitcast(I32),
+            cols = slice(128 * h, 128 * h + 128)
+            for b in range(B):
+                V.quantize_mx(
+                    out=pc[:, b, cols].bitcast(FP8X4), scales=ps[:, b, cols], in_=og[h][:, b].rearrange("p i a w t -> p (i a w t)")
                 )
 
-        make_taps()
-        w_group("z", 1, S)
+        def store_words(h, queue):
+            dst = words[0].rearrange("p (b n) t -> p b (n t)", b=B)[:, :, 512 * h : 512 * h + 512].bitcast(I32)
+            queue.dma_start(out=dst, in_=pc[:, :, 128 * h : 128 * h + 128].bitcast(I32))
+
+        def store_scales(k, queue):
+            cols = slice(0, 512)
+            for quad in range(4):
+                dst = scales[0, 4 * quad : 4 * quad + 4, :].rearrange("q (b n) -> q b n", b=B)[:, :, cols]
+                queue.dma_start(out=dst.bitcast(I32), in_=ps[32 * quad : 32 * quad + 4, :, cols].bitcast(I32))
+
         w_group("z", 0, V)
+        w_group("z", 1, S)
         x_transpose(1)
-        w_negate(0)
-        w_quant("z", 0, 256)
+        make_taps()
         x_transpose(0)
         w_quant("z", 256, 512)
-        x_transpose(2)
-        w_negate(1)
-        x_group(0, S)
         x_group(1, V)
+        x_transpose(2)
+        x_group(0, S)
+        w_negate(0)
         x_transpose(3)
+        w_negate(1)
         x_group(2, S)
+        w_quant("z", 0, 256)
         x_group(3, V)
-        w_group("q", 1, S)
-        x_quant(0)
-        x_quant(1)
         w_group("q", 0, S)
-        transform(0, 1)
         w_quant("zn", 256, 512)
+        x_quant(0)
+        w_group("q", 1, S)
+        x_quant(1)
+        transform(0, 1)
         w_quant("zn", 0, 256)
         transform(0, 2)
         w_group("g1", 1, G)
@@ -393,206 +403,218 @@ def tile_focalmodulationtwolevel_x1_kernel(tc, x, wq, wz, wg, k, g, wh, out, wor
         transform(1, 2)
         product(0, 2, 1)
         mid(0, 1, 0)
-        w_group("g0", 1, S)
-        w_group("g1", 0, G)
-        mid(0, 2, 0)
-        mid(0, 1, 2)
-        mid(0, 2, 2)
-        w_group("g0", 0, S)
-        w_quant("q", 0, 512)
-        transform(2, 2)
-        sum_diff(0, 1)
-        transform(0, 3)
-        product(1, 2, 1)
-        w_quant("g1", 0, 512)
-        q_mm(0, 1)
-        product(1, 2, 2)
-        transform(1, 1)
-        w_quant("g0", 0, 512)
-        product(1, 2, 0)
-        q_mm(0, 0)
-        sum_diff(0, 0)
-        product(1, 1, 1)
-        gate(0, 1, 1)
-        mid(1, 2, 0)
-        chain(0, 1, 1)
         transform(0, 0)
-        product(2, 2, 0)
-        mid(1, 1, 0)
+        w_group("g1", 0, G)
+        w_group("g0", 0, S)
+        mid(0, 2, 0)
+        transform(1, 1)
+        mid(0, 1, 2)
+        transform(0, 3)
+        mid(0, 2, 2)
+        product(1, 1, 1)
+        w_quant("q", 0, 512)
+        product(1, 2, 1)
+        sum_diff(0, 1)
+        w_group("g0", 1, S)
+        q_mm(0, 0)
         transform(2, 1)
-        q_copy(0, 1, S)
-        chain(0, 1, 0)
-        mid(1, 2, 2)
-        product(2, 1, 1)
-        mid(1, 1, 2)
-        product(2, 1, 0)
-        chain(0, 0, 1)
-        sum_diff(1, 1)
-        product(2, 1, 2)
-        chain(0, 1, 2)
+        sum_diff(0, 0)
+        q_mm(0, 1)
+        w_quant("g1", 0, 512)
+        transform(2, 2)
+        product(1, 2, 0)
+        w_quant("g0", 0, 512)
+        product(1, 2, 2)
+        mid(1, 1, 0)
+        mid(1, 2, 0)
         product(2, 2, 1)
-        chain(0, 0, 0)
-        transform(1, 3)
-        sum_diff(1, 0)
-        q_copy(0, 0, S)
-        transform(3, 1)
-        chain(0, 0, 2)
+        chain(0, 1, 1)
         product(2, 2, 2)
-        chain(1, 1, 1)
-        mid(2, 2, 0)
-        transform(1, 0)
-        gelu(0, 0)
-        q_mm(0, 2)
-        chain(1, 1, 0)
-        gate(0, 1, 0)
-        mid(2, 1, 0)
-        q_copy(0, 2, S)
+        mid(1, 1, 2)
+        mid(1, 2, 2)
+        q_copy(0, 0, S)
+        chain(0, 1, 0)
+        product(2, 2, 0)
+        chain(0, 0, 1)
+        sum_diff(1, 0)
+        q_copy(0, 1, S)
         transform(3, 2)
-        chain(1, 0, 1)
-        gelu(0, 1)
+        chain(0, 1, 2)
+        product(2, 1, 1)
+        q_mm(0, 2)
+        chain(0, 0, 0)
+        sum_diff(1, 1)
+        gate(0, 1, 0)
+        q_copy(0, 2, S)
         q_mm(0, 3)
-        chain(1, 1, 2)
-        gate(0, 0, 0)
-        mid(2, 2, 2)
-        chain(1, 0, 0)
-        transform(2, 3)
-        glob_gain(0)
-        product(3, 1, 1)
-        local(0, 0)
+        mid(2, 1, 0)
+        transform(1, 3)
+        product(3, 2, 0)
+        chain(0, 0, 2)
+        mid(2, 2, 0)
+        product(3, 2, 1)
+        chain(1, 1, 1)
+        transform(1, 0)
         q_copy(0, 3, S)
         mid(2, 1, 2)
-        chain(1, 0, 2)
-        q_mm(1, 0)
-        product(3, 2, 1)
+        make_diag(3)
+        chain(1, 0, 1)
+        gelu(0, 1)
         gate(0, 0, 1)
-        mid(3, 1, 0)
-        transform(2, 0)
-        q_copy(1, 0, S)
-        sum_diff(2, 0)
-        local(0, 1)
+        mid(2, 2, 2)
+        gate(0, 0, 0)
+        chain(1, 1, 0)
+        transform(3, 1)
+        gelu(0, 0)
+        chain(1, 0, 0)
+        gate(0, 1, 1)
         product(3, 2, 2)
-        combine(0, 0, 0)
-        gate(1, 0, 0)
-        combine(0, 1, 1)
-        q_mm(1, 1)
-        gelu(1, 1)
-        sum_diff(2, 1)
-        combine(0, 0, 1)
-        mid(3, 1, 2)
-        product(3, 2, 0)
-        chain(2, 0, 1)
-        gelu(1, 0)
         mid(3, 2, 0)
+        chain(1, 1, 2)
+        product(3, 1, 0)
+        local(0, 0)
+        transform(3, 0)
+        sum_diff(2, 1)
+        glob_gain(0)
+        product(3, 1, 1)
+        local(0, 1)
+        transform(2, 3)
+        d0_copy(3)
+        chain(1, 0, 2)
+        q_mm(1, 1)
+        sum_diff(2, 0)
+        q_mm(1, 0)
+        combine(0, 0, 1)
+        product(3, 1, 2)
+        transform(2, 0)
+        combine(0, 1, 1)
+        q_copy(1, 1, S)
         chain(2, 1, 1)
-        w_group("h", 0, S)
+        y0_taps(3)
+        mid(3, 1, 0)
+        gelu(1, 1)
+        chain(2, 0, 1)
         combine(0, 1, 0)
+        q_copy(1, 0, S)
         chain(2, 0, 0)
         mid(3, 2, 2)
+        gelu(1, 0)
         chain(2, 1, 0)
-        q_copy(1, 1, S)
-        local(1, 0)
-        glob_gain(1)
-        sum_diff(3, 0)
-        gate(1, 0, 1)
         chain(2, 0, 2)
-        gate(1, 1, 1)
-        q_mm(1, 2)
-        local(1, 1)
-        transform(3, 0)
-        sum_diff(3, 1)
-        chain(2, 1, 2)
-        gate(1, 1, 0)
-        combine(1, 1, 0)
-        transform(3, 3)
-        gelu(2, 0)
-        chain(3, 0, 1)
-        q_mm(1, 3)
-        combine(1, 1, 1)
-        gelu(2, 1)
-        combine(1, 0, 0)
-        chain(3, 0, 0)
-        q_copy(1, 2, S)
-        chain(3, 1, 1)
-        q_copy(1, 3, S)
-        gate(2, 0, 0)
-        combine(1, 0, 1)
-        gate(2, 1, 1)
-        glob_gain(2)
+        mid(3, 1, 2)
         w_group("h", 1, S)
+        combine(0, 0, 0)
+        chain(2, 1, 2)
+        gate(1, 0, 0)
+        gate(1, 1, 0)
+        sum_diff(3, 1)
+        glob_gain(1)
+        local(1, 0)
+        gate(1, 0, 1)
+        gelu(2, 0)
+        transform(3, 3)
+        local(1, 1)
+        gelu(2, 1)
+        gate(1, 1, 1)
+        sum_diff(3, 0)
+        chain(3, 1, 1)
+        q_mm(1, 3)
+        q_mm(1, 2)
+        combine(1, 1, 1)
+        glob_gain(2)
+        q_copy(1, 3, S)
         chain(3, 1, 0)
+        y0_sum(3)
+        q_copy(1, 2, S)
+        combine(1, 1, 0)
+        combine(1, 0, 0)
+        w_group("h", 0, S)
+        combine(1, 0, 1)
+        gate(2, 0, 0)
+        chain(3, 1, 2)
         gate(2, 0, 1)
         gate(2, 1, 0)
-        chain(3, 0, 2)
         local(2, 0)
+        gelu(3, 0)
+        gate(2, 1, 1)
         local(2, 1)
-        chain(3, 1, 2)
+        combine(2, 0, 1)
+        gelu(3, 1)
         gate(3, 0, 1)
+        combine(2, 0, 0)
         gate(3, 0, 0)
         combine(2, 1, 1)
-        gelu(3, 0)
         combine(2, 1, 0)
-        combine(2, 0, 0)
-        gelu(3, 1)
-        combine(2, 0, 1)
-        w_quant("h", 0, 512)
-        gate(3, 1, 0)
+        zadd(3, 0)
+        zadd(3, 1)
         gate(3, 1, 1)
-        glob_gain(3)
-        local(3, 0)
         local(3, 1)
-        combine(3, 0, 1)
-        combine(3, 0, 0)
+        glob_gain(3)
+        gate(3, 1, 0)
+        w_quant("h", 0, 512)
         combine(3, 1, 0)
-        ctx_group(0, 0, S)
-        ctx_group(0, 1, G)
         combine(3, 1, 1)
+        local(3, 0)
+        ctx_group(1, 0, G)
         ctx_group(1, 1, S)
-        ctx_group(1, 0, V)
-        ctx_group(1, 2, G)
-        ctx_group(0, 3, S)
-        ctx_quant(0, 0)
-        ctx_quant(0, 1)
-        m_mm(0, 0)
+        ctx_group(1, 3, S)
+        combine(3, 0, 0)
         ctx_quant(1, 1)
-        ctx_quant(1, 0)
-        ctx_group(0, 2, V)
-        m_mm(1, 0)
-        modulate(0, 0)
-        m_mm(0, 1)
+        combine(3, 0, 1)
         m_mm(1, 1)
-        ctx_quant(0, 2)
-        modulate(1, 0)
-        turn(0, 0)
-        modulate(0, 1)
-        turn(1, 0)
-        out_group(0, 0, S)
-        ctx_quant(0, 3)
+        ctx_quant(1, 0)
+        ctx_group(0, 1, S)
+        ctx_group(0, 2, G)
+        m_mm(1, 0)
         modulate(1, 1)
-        m_mm(0, 2)
-        out_group(1, 0, S)
-        m_mm(0, 3)
-        ctx_group(1, 3, V)
-        turn(0, 1)
-        planes(0)
-        ctx_quant(1, 2)
-        turn(1, 1)
+        ctx_group(0, 0, S)
+        ctx_quant(0, 1)
         ctx_quant(1, 3)
-        modulate(0, 2)
-        m_mm(1, 2)
-        out_group(1, 1, S)
+        m_mm(0, 1)
+        ctx_quant(0, 2)
+        ctx_group(1, 2, S)
+        ctx_quant(0, 0)
         m_mm(1, 3)
-        modulate(1, 2)
-        turn(0, 2)
+        modulate(0, 1)
+        m_mm(0, 0)
+        ctx_group(0, 3, S)
+        turn(1, 1)
+        modulate(0, 0)
+        store_out(1)
+        turn(0, 1)
+        modulate(1, 0)
+        out_group(1, 1, S)
+        turn(0, 0)
+        ctx_quant(0, 3)
         out_group(0, 1, S)
-        modulate(0, 3)
-        turn(1, 2)
-        out_group(0, 2, S)
-        turn(0, 3)
+        store_out(0)
         modulate(1, 3)
-        out_group(1, 2, S)
+        m_mm(0, 3)
+        m_mm(0, 2)
+        ctx_quant(1, 2)
+        out_group(0, 0, S)
         planes(1)
+        turn(1, 0)
+        modulate(0, 3)
+        store_words(1, nc.sync)
+        m_mm(1, 2)
+        modulate(0, 2)
+        out_group(1, 0, S)
         turn(1, 3)
-        out_group(0, 3, S)
-        planes(2)
+        store_out(3)
+        planes(0)
+        turn(0, 2)
+        modulate(1, 2)
+        store_words(0, nc.sync)
+        turn(0, 3)
+        out_group(0, 2, S)
+        store_out(2)
+        turn(1, 2)
         out_group(1, 3, S)
+        out_group(0, 3, S)
         planes(3)
+        out_group(1, 2, S)
+        planes(2)
+        store_words(2, nc.sync)
+        store_words(3, nc.sync)
+        store_scales(0, nc.sync)

from contextlib import ExitStack

import concourse.mybir as mybir
from concourse.masks import make_identity

F32 = mybir.dt.float32
BF16 = mybir.dt.bfloat16
U32 = mybir.dt.uint32
I32 = mybir.dt.int32
U8 = mybir.dt.uint8
FP8X4 = mybir.dt.float8_e4m3fn_x4
ALU = mybir.AluOpType
ACT = mybir.ActivationFunctionType

FLOPS = 5 * 2 * 1024 * 512 * 512

P = 128
B, R, W, C = 2, 16, 32, 512
T = 4
POS = 512
E_COL, O_COL = 0, 576
WIN_E, WIN_E1, WIN_O1, WIN_O = 0, 64, 512, 576
M1 = ("V", "V", "V", "G")
M2 = ("V", "G", "G", "G")
SD = ("V", "G", "G", "G")
Y0 = ("V", "V", "V", "PE")
Q_BANK = (('a0', 'a1', 'a0', 'a1'), ('a0', 'a1', 'a0', 'a1'))
Y0_BANK = "d1"


def tile_focalmodulationtwolevel_x1_kernel(tc, x, wq, wz, wg, k, g, wh, out, words, scales):
    nc = tc.nc
    V, S, G, PE = nc.vector, nc.scalar, nc.gpsimd, nc.tensor

    with ExitStack() as ctx:
        keep = ctx.enter_context(tc.tile_pool(name="keep", bufs=1))
        work = ctx.enter_context(tc.tile_pool(name="work", bufs=2))
        psum = ctx.enter_context(tc.psum_pool(name="psum", bufs=1))
        ctx.enter_context(tc.manual_schedule(engines={mybir.EngineType.PE, mybir.EngineType.Activation, mybir.EngineType.DVE, mybir.EngineType.Pool}))

        def kt(shape, dtype, name):
            return keep.tile(shape, dtype, name=name, align_bytes=64)

        def wt(shape, dtype, name, bufs=2):
            return work.tile(shape, dtype, name=name, tag=name, bufs=bufs, align_bytes=64)

        def bank(name, tag, bufs):
            return psum.tile([P, 512], F32, name=name, tag=tag, bufs=bufs)

        x_tok = x.rearrange("b r w c -> (b r w) c")
        x_sb = kt([P, B, 4, C], BF16, "x_sb")
        taps_bf = kt([P, 3, 3, T], BF16, "taps_bf")
        gain_bf = kt([P, T], BF16, "gain_bf")
        raw = {n: kt([P, 4, C], BF16, "raw_" + n) for n in ("z", "g0", "g1", "q", "h")}

        def load_x(b, half):
            src = x_tok[b * 512 + half * 256 : b * 512 + half * 256 + 256, :]
            nc.sync.dma_start(out=x_sb[:, b, 2 * half : 2 * half + 2, :], in_=src.rearrange("(q p) c -> p q c", p=P))

        def load_w(n, ap):
            nc.sync.dma_start(out=raw[n][:], in_=ap.rearrange("(p j) n -> p j n", j=4))

        nc.scalar.dma_start(out=taps_bf[:], in_=k.rearrange("u v (p t) -> p (u v) t", t=T).rearrange("p (u v) t -> p u v t", u=3))
        nc.scalar.dma_start(out=gain_bf[:], in_=g.rearrange("(p t) -> p t", t=T))
        load_w("z", wz)
        load_x(0, 0)
        load_x(1, 0)
        load_x(0, 1)
        load_x(1, 1)
        load_w("q", wq)
        load_w("g0", wg[0])
        load_w("g1", wg[1])
        load_w("h", wh)

        ident = kt([P, P], F32, "ident")
        make_identity(nc, ident[:])
        xg = kt([P, 2, POS, 4], BF16, "xg")
        xc = kt([P, 1088], U32, "xc")
        xs = kt([P, 1088], U8, "xs")
        V.memset(xc[:, 512:576], 0)
        V.memset(xs[:, 512:576].bitcast(U32), 0)
        warm = kt([P, 1], F32, "warm")
        warm2 = kt([P, 1], F32, "warm2")
        V.memset(warm[:], 0.0)
        S.activation(out=warm2[:], in_=warm[:], func=ACT.Gelu_apprx_tanh)

        taps = kt([P, 4, 3, T], F32, "taps")
        outer_half = kt([P, 3, T], F32, "outer_half")
        gain = kt([P, T], F32, "gain")
        gain_mean = kt([P, T], F32, "gain_mean")

        def make_taps():
            V.tensor_tensor(out=outer_half[:], in0=taps_bf[:, 0], in1=taps_bf[:, 2], op=ALU.add)
            V.tensor_copy(out=taps[:, 0], in_=taps_bf[:, 0])
            V.tensor_scalar(out=taps[:, 3], in0=taps_bf[:, 2], scalar1=-1.0, scalar2=None, op0=ALU.mult)
            V.tensor_scalar(out=outer_half[:], in0=outer_half[:], scalar1=0.5, scalar2=None, op0=ALU.mult)
            V.tensor_copy(out=gain[:], in_=gain_bf[:])
            V.tensor_scalar(out=gain_mean[:], in0=gain_bf[:], scalar1=1.0 / 512, scalar2=None, op0=ALU.mult)
            V.scalar_tensor_tensor(out=taps[:, 1], in0=taps_bf[:, 1], scalar=0.5, in1=outer_half[:], op0=ALU.mult, op1=ALU.add)
            V.scalar_tensor_tensor(out=taps[:, 2], in0=taps_bf[:, 1], scalar=-0.5, in1=outer_half[:], op0=ALU.mult, op1=ALU.add)

        def copy_on(eng, dst, src):
            if eng is S:
                S.copy(out=dst, in_=src)
            elif eng is V:
                V.tensor_copy(out=dst, in_=src)
            else:
                G.tensor_scalar(out=dst, in0=src, scalar1=1.0, scalar2=0.0, op0=ALU.mult, op1=ALU.add)

        xt_tiles = {}

        def x_transpose(q):
            xt = psum.tile([P, 2, 2, 2, B, W], F32, name="xt%d" % q, tag="a%d" % q, bufs=1)
            xt_tiles[q] = xt
            for b in range(B):
                blk = x_sb[:, b, q, :].bitcast(F32)
                for u in range(2):
                    PE.transpose(xt[:, u, :, :, b, :].rearrange("p a i w -> p i a w"), blk[:, u:256:2], ident[:])

        def x_group(q, eng):
            dst = xg[:, :, 128 * q : 128 * q + 128, :].rearrange("p a n j -> p a (n j)").bitcast(F32)
            copy_on(eng, dst.rearrange("p a (n u) -> p a n u", u=2), xt_tiles[q][:].rearrange("p u a i b w -> p a (i b w) u"))

        def x_quant(par):
            c0 = (E_COL, O_COL)[par]
            V.quantize_mx(
                out=xc[:, c0 : c0 + POS].bitcast(FP8X4),
                scales=xs[:, c0 : c0 + POS],
                in_=xg[:, par, :, :].rearrange("p n j -> p (n j)"),
            )

        grp = {n: kt([P, 2048], BF16, "grp_" + n) for n in ("z", "zn", "g0", "g1", "q", "h")}
        wc = {n: kt([P, 512], U32, "wc_" + n) for n in ("z", "zn", "g0", "g1", "q", "h")}
        ws = {n: kt([P, 512], U8, "ws_" + n) for n in ("z", "zn", "g0", "g1", "q", "h")}

        def w_group(n, half, eng):
            if n in ("z", "g0", "g1"):
                src = raw[n][:].rearrange("p j (m t) -> p t m j", t=T)[:, 2 * half : 2 * half + 2]
                dst = grp[n][:].rearrange("p (t m j) -> p t m j", t=T, j=4)[:, 2 * half : 2 * half + 2]
            else:
                src = raw[n][:].rearrange("p j n -> p n j")[:, 256 * half : 256 * half + 256]
                dst = grp[n][:].rearrange("p (n j) -> p n j", j=4)[:, 256 * half : 256 * half + 256]
            copy_on(eng, dst, src)

        def w_negate(half):
            sl = slice(1024 * half, 1024 * half + 1024)
            V.tensor_scalar(out=grp["zn"][:, sl], in0=grp["z"][:, sl], scalar1=-1.0, scalar2=None, op0=ALU.mult)

        def w_quant(n, lo, hi):
            V.quantize_mx(out=wc[n][:, lo:hi].bitcast(FP8X4), scales=ws[n][:, lo:hi], in_=grp[n][:, 4 * lo : 4 * hi])

        def mm(o, n, t, win, start, stop):
            c = 128 * t
            PE.matmul_mx(
                out=o[:],
                lhsT=wc[n][:, c : c + 128].bitcast(FP8X4),
                lhsT_scale=ws[n][:, c : c + 128],
                rhs=xc[:, win : win + POS].bitcast(FP8X4),
                rhs_scale=xs[:, win : win + POS],
                start=start,
                stop=stop,
            )

        d, prod, y, z1, zsum, gz, a = ({} for i in range(7))
        tmp, zpart = {}, {}
        cf = kt([P, T, 2, POS], F32, "cf")

        def grid(ap):
            return ap.rearrange("p (n w) -> p n w", w=W)

        def transform(t, i):
            d[t, i] = bank("d%d_%d" % (i, t), "a%d" % (i + 1) if t == 1 and i in (1, 2) else "d2" if i == 0 and Y0[t] == "PE" else "d%d" % i, 1)
            first, second, name = ((WIN_O1, WIN_O, "zn"), (WIN_E, WIN_O, "z"), (WIN_O, WIN_E, "zn"), (WIN_E, WIN_E1, "zn"))[i]
            mm(d[t, i], "z", t, first, True, False)
            mm(d[t, i], name, t, second, False, True)

        def gate(t, which, par):
            for win in ((WIN_E, WIN_O)[par],):
                a[t, which, par] = bank("a%d%d_%d" % (which, par, t), "a%d" % (2 * which + par), 1)
                mm(a[t, which, par], "g%d" % which, t, win, True, True)

        SPAN = ((slice(1, W), slice(0, W - 1)), (slice(0, W), slice(0, W)), (slice(0, W - 1), slice(1, W)))

        def product(t, i, v):
            if (t, v) not in prod:
                prod[t, v] = wt([P, 2, 16, W], F32, "prod%d" % v)
            dst, src = SPAN[v]
            S.activation(
                out=prod[t, v][:, i - 1, :, dst], in_=grid(d[t, i][:])[:, :, src], func=ACT.Copy, scale=taps[:, i, v, t : t + 1]
            )

        def products(t):
            for i in (1, 2):
                product(t, i, 1)
                if (M1, M2)[i - 1][t] == "G":
                    product(t, i, 0)
                    product(t, i, 2)

        def fused(t, i, v, o):
            dst, src = SPAN[v]
            V.scalar_tensor_tensor(
                out=o[:, :, dst], in0=grid(d[t, i][:])[:, :, src], scalar=taps[:, i, v, t : t + 1], in1=o[:, :, dst], op0=ALU.mult, op1=ALU.add
            )

        def mid(t, i, v):
            acc = prod[t, 1]
            dst = SPAN[v][0]
            if (M1, M2)[i - 1][t] == "V":
                fused(t, i, v, acc[:, i - 1])
            else:
                G.tensor_tensor(out=acc[:, i - 1, :, dst], in0=acc[:, i - 1, :, dst], in1=prod[t, v][:, i - 1, :, dst], op=ALU.add)

        def sum_diff(t, half):
            acc = prod[t, 1]
            if t not in y:
                y[t] = wt([P, 2, 16, W], F32, "y")
            eng = V if SD[t] == "V" else G
            eng.tensor_tensor(out=y[t][:, half], in0=acc[:, 0], in1=acc[:, 1], op=(ALU.add, ALU.subtract)[half])

        def chain(t, half, v):
            fused(t, (0, 3)[half], v, y[t][:, half])

        diag = {}

        def make_diag(t):
            for v in range(3):
                diag[t, v] = kt([P, P], F32, "diag%d%d" % (t, v))
                G.tensor_scalar(out=diag[t, v][:], in0=ident[:], scalar1=taps[:, 0, v, t : t + 1], scalar2=0.0, op0=ALU.mult, op1=ALU.add)

        d0_sb, y0 = {}, {}

        def d0_copy(t):
            d0_sb[t] = wt([P, 16, W], F32, "d0_sb")
            S.copy(out=d0_sb[t][:], in_=grid(d[t, 0][:]))

        def y0_taps(t):
            y0[t] = bank("y0_%d" % t, Y0_BANK, 1)
            PE.matmul(out=y0[t][:], lhsT=diag[t, 1][:], rhs=d0_sb[t][:].rearrange("p n w -> p (n w)"), start=True, stop=False)
            for v in (0, 2):
                dst, src = SPAN[v]
                PE.matmul(out=grid(y0[t][:])[:, :, dst], lhsT=diag[t, v][:], rhs=d0_sb[t][:, :, src], start=False, stop=False)

        def y0_sum(t):
            PE.matmul(out=y0[t][:], lhsT=ident[:], rhs=y[t][:, 0].rearrange("p n w -> p (n w)"), start=False, stop=True)

        def of_batch(ap, b):
            return ap.rearrange("p (n b w) -> p n b w", b=B, w=W)[:, :, b, :]

        def gelu(t, b):
            if t not in z1:
                z1[t] = wt([P, 2 * POS], F32, "z1")
                zsum[t] = wt([P, B], F32, "zsum")
                gz[t] = wt([P, B], F32, "gz")
            if Y0[t] == "PE":
                for par, src in enumerate((y0[t][:], y[t][:, 1].rearrange("p n w -> p (n w)"))):
                    if (t, b) not in zpart:
                        zpart[t, b] = wt([P, 2], F32, "zpart%d" % b)
                    S.activation(
                        out=of_batch(z1[t][:, par * POS : (par + 1) * POS], b),
                        in_=of_batch(src, b),
                        func=ACT.Gelu_apprx_tanh,
                        accum_out=zpart[t, b][:, par : par + 1],
                    )
                return
            S.activation(
                out=of_batch(z1[t][:], b),
                in_=of_batch(y[t][:].rearrange("p a n w -> p (a n w)"), b),
                func=ACT.Gelu_apprx_tanh,
                accum_out=zsum[t][:, b : b + 1],
            )

        def zadd(t, b):
            V.tensor_tensor(out=zsum[t][:, b : b + 1], in0=zpart[t, b][:, 0:1], in1=zpart[t, b][:, 1:2], op=ALU.add)

        def glob_gain(t):
            S.activation(out=gz[t][:], in_=zsum[t][:], func=ACT.Copy, scale=gain_mean[:, t : t + 1])

        def local(t, par):
            if t not in tmp:
                tmp[t] = wt([P, 2, POS], F32, "tmp", bufs=1)
            V.scalar_tensor_tensor(
                out=tmp[t][:, par], in0=z1[t][:, par * POS : (par + 1) * POS], scalar=gain[:, t : t + 1], in1=a[t, 0, par][:], op0=ALU.mult, op1=ALU.mult
            )

        def combine(t, par, b):
            V.scalar_tensor_tensor(
                out=of_batch(cf[:, t, par, :], b), in0=of_batch(a[t, 1, par][:], b), scalar=gz[t][:, b : b + 1], in1=of_batch(tmp[t][:, par], b), op0=ALU.mult, op1=ALU.add
            )

        q_sb = kt([P, 2, 4, C], F32, "q_sb")
        qb = {}

        def q_mm(par, h):
            c0 = (E_COL, O_COL)[par] + 128 * h
            qb[par, h] = bank("q%d%d" % (par, h), Q_BANK[par][h], 1)
            PE.matmul_mx(
                out=qb[par, h][:],
                lhsT=xc[:, c0 : c0 + 128].bitcast(FP8X4),
                lhsT_scale=xs[:, c0 : c0 + 128],
                rhs=wc["q"][:].bitcast(FP8X4),
                rhs_scale=ws["q"][:],
                start=True,
                stop=True,
            )

        def q_copy(par, h, eng):
            copy_on(eng, q_sb[:, par, h, :], qb[par, h][:])

        ctxg = kt([P, 2, POS, 4], BF16, "ctxg")
        cc = kt([P, 2, POS], U32, "cc")
        cs = kt([P, 2, POS], U8, "cs")
        og, o_sb, m_bank, ot = {}, {}, {}, {}

        def ctx_group(par, h, eng):
            sl = slice(128 * h, 128 * h + 128)
            copy_on(eng, ctxg[:, par, sl, :], cf[:, :, par, sl].rearrange("p t n -> p n t"))

        def ctx_quant(par, h):
            sl = slice(128 * h, 128 * h + 128)
            V.quantize_mx(out=cc[:, par, sl].bitcast(FP8X4), scales=cs[:, par, sl], in_=ctxg[:, par, sl, :].rearrange("p n t -> p (n t)"))

        def m_mm(par, h):
            sl = slice(128 * h, 128 * h + 128)
            m_bank[par, h] = bank("m%d%d" % (par, h), "a%d" % (2 * (h % 2) + par), 1)
            PE.matmul_mx(
                out=m_bank[par, h][:],
                lhsT=cc[:, par, sl].bitcast(FP8X4),
                lhsT_scale=cs[:, par, sl],
                rhs=wc["h"][:].bitcast(FP8X4),
                rhs_scale=ws["h"][:],
                start=True,
                stop=True,
            )

        def modulate(par, h):
            if h not in o_sb:
                o_sb[h] = wt([P, 2, C], F32, "o", bufs=4)
            V.tensor_tensor(out=o_sb[h][:, par, :], in0=m_bank[par, h][:], in1=q_sb[:, par, h, :], op=ALU.mult)

        def store_out(h):
            for i in range(2):
                for b in range(B):
                    lo = 64 * i + 32 * b
                    dst = out[b, 4 * h + 2 * i : 4 * h + 2 * i + 2, :, :].rearrange("a w n -> w a n")
                    nc.sync.dma_start(out=dst, in_=o_sb[h][lo : lo + 32, :, :])

        def turn(par, h):
            ot[par, h] = psum.tile([P, T, 2, B, W], F32, name="ot%d%d" % (par, h), tag="d%d" % (2 * (h % 2) + par), bufs=1)
            for t in range(T):
                PE.transpose(ot[par, h][:, t].rearrange("p i b w -> p (i b w)"), o_sb[h][:, par, t:C:4], ident[:])

        def out_group(par, h, eng):
            if h not in og:
                og[h] = kt([P, B, 2, 2, W, 4], BF16, "og%d" % h)
            for b in range(B):
                copy_on(eng, og[h][:, b, :, par, :, :], ot[par, h][:, :, :, b, :].rearrange("p t i w -> p i w t"))

        pc = kt([P, B, 512], U32, "pc")
        ps = kt([P, B, 512], U8, "ps")

        def planes(h):
            cols = slice(128 * h, 128 * h + 128)
            for b in range(B):
                V.quantize_mx(
                    out=pc[:, b, cols].bitcast(FP8X4), scales=ps[:, b, cols], in_=og[h][:, b].rearrange("p i a w t -> p (i a w t)")
                )

        def store_words(h, queue):
            dst = words[0].rearrange("p (b n) t -> p b (n t)", b=B)[:, :, 512 * h : 512 * h + 512].bitcast(I32)
            queue.dma_start(out=dst, in_=pc[:, :, 128 * h : 128 * h + 128].bitcast(I32))

        def store_scales(k, queue):
            cols = slice(0, 512)
            for quad in range(4):
                dst = scales[0, 4 * quad : 4 * quad + 4, :].rearrange("q (b n) -> q b n", b=B)[:, :, cols]
                queue.dma_start(out=dst.bitcast(I32), in_=ps[32 * quad : 32 * quad + 4, :, cols].bitcast(I32))

        w_group("z", 0, V)
        w_group("z", 1, S)
        x_transpose(1)
        make_taps()
        x_transpose(0)
        w_quant("z", 256, 512)
        x_group(1, V)
        x_transpose(2)
        x_group(0, S)
        w_negate(0)
        x_transpose(3)
        w_negate(1)
        x_group(2, S)
        w_quant("z", 0, 256)
        x_group(3, V)
        w_group("q", 0, S)
        w_quant("zn", 256, 512)
        x_quant(0)
        w_group("q", 1, S)
        x_quant(1)
        transform(0, 1)
        w_quant("zn", 0, 256)
        transform(0, 2)
        w_group("g1", 1, G)
        product(0, 1, 1)
        transform(1, 2)
        product(0, 2, 1)
        mid(0, 1, 0)
        transform(0, 0)
        w_group("g1", 0, G)
        w_group("g0", 0, S)
        mid(0, 2, 0)
        transform(1, 1)
        mid(0, 1, 2)
        transform(0, 3)
        mid(0, 2, 2)
        product(1, 1, 1)
        w_quant("q", 0, 512)
        product(1, 2, 1)
        sum_diff(0, 1)
        w_group("g0", 1, S)
        q_mm(0, 0)
        transform(2, 1)
        sum_diff(0, 0)
        q_mm(0, 1)
        w_quant("g1", 0, 512)
        transform(2, 2)
        product(1, 2, 0)
        w_quant("g0", 0, 512)
        product(1, 2, 2)
        mid(1, 1, 0)
        mid(1, 2, 0)
        product(2, 2, 1)
        chain(0, 1, 1)
        product(2, 2, 2)
        mid(1, 1, 2)
        mid(1, 2, 2)
        q_copy(0, 0, S)
        chain(0, 1, 0)
        product(2, 2, 0)
        chain(0, 0, 1)
        sum_diff(1, 0)
        q_copy(0, 1, S)
        transform(3, 2)
        chain(0, 1, 2)
        product(2, 1, 1)
        q_mm(0, 2)
        chain(0, 0, 0)
        sum_diff(1, 1)
        gate(0, 1, 0)
        q_copy(0, 2, S)
        q_mm(0, 3)
        mid(2, 1, 0)
        transform(1, 3)
        product(3, 2, 0)
        chain(0, 0, 2)
        mid(2, 2, 0)
        product(3, 2, 1)
        chain(1, 1, 1)
        transform(1, 0)
        q_copy(0, 3, S)
        mid(2, 1, 2)
        make_diag(3)
        chain(1, 0, 1)
        gelu(0, 1)
        gate(0, 0, 1)
        mid(2, 2, 2)
        gate(0, 0, 0)
        chain(1, 1, 0)
        transform(3, 1)
        gelu(0, 0)
        chain(1, 0, 0)
        gate(0, 1, 1)
        product(3, 2, 2)
        mid(3, 2, 0)
        chain(1, 1, 2)
        product(3, 1, 0)
        local(0, 0)
        transform(3, 0)
        sum_diff(2, 1)
        glob_gain(0)
        product(3, 1, 1)
        local(0, 1)
        transform(2, 3)
        d0_copy(3)
        chain(1, 0, 2)
        q_mm(1, 1)
        sum_diff(2, 0)
        q_mm(1, 0)
        combine(0, 0, 1)
        product(3, 1, 2)
        transform(2, 0)
        combine(0, 1, 1)
        q_copy(1, 1, S)
        chain(2, 1, 1)
        y0_taps(3)
        mid(3, 1, 0)
        gelu(1, 1)
        chain(2, 0, 1)
        combine(0, 1, 0)
        q_copy(1, 0, S)
        chain(2, 0, 0)
        mid(3, 2, 2)
        gelu(1, 0)
        chain(2, 1, 0)
        chain(2, 0, 2)
        mid(3, 1, 2)
        w_group("h", 1, S)
        combine(0, 0, 0)
        chain(2, 1, 2)
        gate(1, 0, 0)
        gate(1, 1, 0)
        sum_diff(3, 1)
        glob_gain(1)
        local(1, 0)
        gate(1, 0, 1)
        gelu(2, 0)
        transform(3, 3)
        local(1, 1)
        gelu(2, 1)
        gate(1, 1, 1)
        sum_diff(3, 0)
        chain(3, 1, 1)
        q_mm(1, 3)
        q_mm(1, 2)
        combine(1, 1, 1)
        glob_gain(2)
        q_copy(1, 3, S)
        chain(3, 1, 0)
        y0_sum(3)
        q_copy(1, 2, S)
        combine(1, 1, 0)
        combine(1, 0, 0)
        w_group("h", 0, S)
        combine(1, 0, 1)
        gate(2, 0, 0)
        chain(3, 1, 2)
        gate(2, 0, 1)
        gate(2, 1, 0)
        local(2, 0)
        gelu(3, 0)
        gate(2, 1, 1)
        local(2, 1)
        combine(2, 0, 1)
        gelu(3, 1)
        gate(3, 0, 1)
        combine(2, 0, 0)
        gate(3, 0, 0)
        combine(2, 1, 1)
        combine(2, 1, 0)
        zadd(3, 0)
        zadd(3, 1)
        gate(3, 1, 1)
        local(3, 1)
        glob_gain(3)
        gate(3, 1, 0)
        w_quant("h", 0, 512)
        combine(3, 1, 0)
        combine(3, 1, 1)
        local(3, 0)
        ctx_group(1, 0, G)
        ctx_group(1, 1, S)
        ctx_group(1, 3, S)
        combine(3, 0, 0)
        ctx_quant(1, 1)
        combine(3, 0, 1)
        m_mm(1, 1)
        ctx_quant(1, 0)
        ctx_group(0, 1, S)
        ctx_group(0, 2, G)
        m_mm(1, 0)
        modulate(1, 1)
        ctx_group(0, 0, S)
        ctx_quant(0, 1)
        ctx_quant(1, 3)
        m_mm(0, 1)
        ctx_quant(0, 2)
        ctx_group(1, 2, S)
        ctx_quant(0, 0)
        m_mm(1, 3)
        modulate(0, 1)
        m_mm(0, 0)
        ctx_group(0, 3, S)
        turn(1, 1)
        modulate(0, 0)
        store_out(1)
        turn(0, 1)
        modulate(1, 0)
        out_group(1, 1, S)
        turn(0, 0)
        ctx_quant(0, 3)
        out_group(0, 1, S)
        store_out(0)
        modulate(1, 3)
        m_mm(0, 3)
        m_mm(0, 2)
        ctx_quant(1, 2)
        out_group(0, 0, S)
        planes(1)
        turn(1, 0)
        modulate(0, 3)
        store_words(1, nc.sync)
        m_mm(1, 2)
        modulate(0, 2)
        out_group(1, 0, S)
        turn(1, 3)
        store_out(3)
        planes(0)
        turn(0, 2)
        modulate(1, 2)
        store_words(0, nc.sync)
        turn(0, 3)
        out_group(0, 2, S)
        store_out(2)
        turn(1, 2)
        out_group(1, 3, S)
        out_group(0, 3, S)
        planes(3)
        out_group(1, 2, S)
        planes(2)
        store_words(2, nc.sync)
        store_words(3, nc.sync)
        store_scales(0, nc.sync)
